import numpy as np
CORES = [0,9,18,27,36,45,54,63,64,73,82,91,100,109,118,127]
N = 16
T, K = 128, 3
ROUTE = [[[6,11,12],[9,15,14],[12,1,2],[7,1,14],[12,4,13],[8,1,11],[14,9,5],[13,11,15],[7,5,13],[8,13,10],[0,11,3],[10,14,9],[12,0,14],[5,13,1],[13,15,2],[10,6,8],[6,1,4],[9,0,11],[0,4,1],[13,0,9],[1,0,13],[13,5,0],[6,12,7],[10,4,11],[0,12,9],[6,0,7],[3,5,15],[8,1,2],[3,13,8],[8,12,11],[6,14,8],[2,4,14],[15,12,6],[1,14,2],[8,13,10],[9,8,5],[4,1,8],[1,8,5],[2,12,7],[10,12,15],[6,14,10],[5,14,7],[9,0,4],[4,5,10],[0,10,15],[2,14,1],[2,4,13],[14,7,8],[3,1,11],[15,2,8],[4,1,9],[8,3,9],[6,8,2],[10,12,4],[8,11,2],[11,8,15],[4,12,10],[2,13,11],[6,13,1],[15,14,1],[9,6,4],[4,11,12],[0,6,12],[4,2,12],[0,8,2],[12,11,2],[10,7,2],[12,2,7],[12,11,2],[7,3,2],[9,1,6],[15,5,12],[0,10,3],[2,15,3],[14,11,10],[5,15,9],[8,7,15],[10,7,14],[8,5,15],[3,11,2],[12,15,7],[10,13,5],[11,6,10],[15,2,5],[12,13,9],[1,2,0],[6,5,7],[4,6,14],[14,10,0],[7,0,5],[7,3,13],[12,8,7],[3,13,12],[14,4,15],[13,12,10],[15,0,5],[9,15,2],[4,7,13],[1,9,6],[10,13,11],[13,11,1],[15,0,2],[3,1,13],[14,6,8],[15,2,3],[7,11,13],[12,9,5],[12,5,2],[8,4,14],[5,7,2],[2,12,0],[10,4,11],[1,14,8],[2,11,0],[3,10,2],[3,11,4],[8,15,6],[2,1,5],[11,6,13],[3,0,14],[0,12,5],[2,3,11],[10,2,0],[12,2,11],[5,2,15],[11,15,5],[10,11,15],[4,13,8]],[[4,1,12],[9,7,0],[12,0,14],[10,6,7],[7,9,10],[9,2,6],[1,6,0],[10,3,13],[11,8,9],[2,7,14],[14,6,12],[10,5,2],[8,0,12],[1,15,10],[15,14,10],[15,3,7],[14,7,1],[0,9,14],[3,15,14],[11,12,5],[4,13,2],[12,8,4],[1,10,7],[13,4,0],[10,8,11],[3,4,13],[12,4,15],[14,0,1],[13,8,0],[11,5,14],[7,4,15],[7,6,1],[4,15,5],[5,15,6],[8,2,6],[7,1,13],[15,5,4],[0,11,7],[13,10,6],[5,1,4],[13,12,4],[9,8,14],[9,0,3],[4,12,9],[1,5,0],[7,6,2],[0,3,13],[15,12,9],[5,6,1],[3,9,4],[13,2,9],[4,6,1],[15,13,8],[1,11,13],[2,1,14],[13,4,15],[5,2,1],[7,9,1],[5,9,13],[11,13,14],[5,14,2],[6,12,13],[11,5,12],[7,8,12],[0,8,11],[2,9,8],[7,0,15],[9,15,11],[6,4,13],[0,7,13],[9,6,4],[14,15,12],[14,4,8],[6,13,9],[4,3,5],[8,13,14],[11,14,10],[12,3,15],[13,15,1],[7,4,2],[14,0,13],[15,13,3],[14,4,0],[11,10,9],[4,2,15],[3,0,9],[12,2,5],[14,4,12],[7,0,2],[0,13,1],[3,8,5],[5,15,8],[5,2,3],[10,5,15],[8,7,11],[4,6,12],[11,0,10],[2,12,13],[2,0,1],[3,11,14],[11,9,10],[7,3,12],[15,2,3],[10,2,13],[9,10,15],[4,11,15],[0,14,12],[10,1,5],[9,5,6],[13,2,0],[11,5,15],[8,2,5],[1,11,15],[15,13,7],[6,14,1],[3,7,11],[6,2,8],[5,7,0],[15,2,0],[9,7,15],[13,9,15],[15,5,0],[14,15,12],[1,11,3],[13,8,7],[11,7,14],[3,11,8],[11,9,3]],[[14,9,8],[8,5,12],[9,5,10],[13,7,10],[7,5,9],[6,7,14],[6,14,11],[5,3,13],[6,15,4],[8,10,15],[7,15,3],[6,11,1],[0,4,11],[4,11,3],[3,12,9],[0,3,2],[10,14,9],[7,2,0],[14,15,5],[7,10,5],[7,12,5],[8,0,3],[5,12,14],[10,8,0],[1,12,8],[11,12,8],[13,2,6],[8,12,14],[5,3,2],[0,5,15],[10,0,15],[3,12,7],[1,4,9],[5,4,14],[15,1,4],[14,2,3],[12,0,9],[5,7,9],[12,11,2],[8,9,3],[7,10,6],[0,3,6],[12,8,1],[2,5,6],[0,11,15],[7,11,14],[5,13,9],[8,6,13],[4,2,8],[9,5,8],[4,5,9],[9,3,0],[2,13,11],[10,9,15],[1,11,5],[9,2,14],[4,7,1],[14,1,2],[10,13,12],[8,3,7],[14,3,12],[0,12,11],[1,6,11],[15,8,6],[3,0,2],[5,3,12],[11,7,8],[13,4,9],[7,15,6],[7,15,0],[3,10,12],[7,0,9],[10,1,0],[5,3,8],[1,10,15],[6,4,9],[8,5,2],[12,9,2],[7,2,4],[1,0,6],[12,15,11],[10,8,1],[7,2,11],[2,1,11],[1,14,4],[12,1,8],[5,0,15],[4,6,13],[12,6,11],[15,4,11],[2,9,14],[8,9,6],[15,9,13],[10,9,12],[4,12,9],[7,2,13],[5,9,3],[0,2,13],[12,8,2],[6,8,3],[10,0,4],[15,12,1],[4,0,7],[15,1,3],[7,0,12],[5,11,3],[1,3,4],[10,4,9],[7,3,15],[11,6,13],[1,3,14],[3,6,15],[5,12,2],[12,13,15],[8,15,9],[2,6,3],[15,13,9],[4,3,12],[3,8,1],[3,9,6],[12,7,6],[8,2,13],[3,11,4],[15,13,5],[14,10,12],[11,2,8],[6,15,4],[12,4,0]],[[1,3,6],[7,5,12],[0,4,15],[6,2,7],[2,5,11],[11,14,3],[10,1,12],[4,9,14],[15,8,3],[9,4,7],[9,3,13],[5,0,8],[9,6,8],[11,14,3],[7,12,4],[9,10,2],[13,4,15],[12,13,6],[6,7,10],[1,11,3],[14,9,0],[14,0,12],[2,15,14],[7,5,3],[9,7,10],[6,2,9],[1,7,3],[1,7,9],[7,4,0],[2,10,15],[10,13,7],[9,11,5],[11,13,14],[5,7,14],[15,3,13],[13,15,1],[9,13,15],[11,3,9],[7,14,0],[6,2,10],[13,12,2],[10,9,4],[5,0,14],[15,1,8],[3,6,14],[7,12,11],[2,10,12],[14,4,2],[12,1,7],[7,14,0],[14,2,4],[11,6,13],[10,7,3],[7,12,3],[4,12,2],[13,15,8],[8,5,3],[5,14,0],[6,8,11],[15,14,11],[4,2,0],[9,15,13],[12,13,9],[10,9,0],[11,10,4],[9,13,1],[6,11,15],[9,6,7],[1,11,5],[1,9,14],[5,13,11],[4,12,13],[9,0,6],[4,7,13],[6,15,12],[2,8,1],[5,2,11],[1,4,6],[0,3,14],[1,15,10],[4,8,7],[1,6,5],[4,8,7],[15,4,7],[11,0,15],[13,5,10],[9,6,7],[14,6,1],[10,15,7],[14,13,2],[8,12,7],[10,4,7],[13,3,4],[14,10,0],[14,4,10],[11,10,8],[2,4,5],[7,10,12],[15,0,7],[14,2,6],[12,13,3],[9,6,15],[5,15,2],[15,9,6],[15,12,6],[11,4,8],[0,11,13],[1,3,12],[13,0,8],[8,9,7],[4,12,10],[9,15,4],[2,0,6],[4,6,10],[0,1,12],[9,5,15],[1,6,13],[10,14,9],[12,1,6],[14,0,1],[7,8,15],[3,10,14],[1,8,0],[12,10,9],[15,14,4],[7,11,8],[1,10,15],[2,10,12]],[[6,2,12],[9,6,15],[3,10,2],[1,8,14],[6,14,5],[1,9,8],[0,5,12],[1,10,4],[13,12,1],[5,14,8],[10,13,15],[14,13,9],[6,3,11],[3,6,13],[14,2,11],[14,2,4],[11,13,2],[5,14,8],[15,11,6],[7,3,11],[2,0,8],[4,15,7],[9,12,11],[15,11,2],[0,10,5],[3,13,14],[15,10,5],[7,1,11],[13,15,6],[3,1,7],[10,14,4],[14,12,6],[11,15,9],[12,11,8],[10,0,2],[5,9,0],[3,14,7],[13,9,3],[0,11,2],[0,14,4],[9,11,3],[9,10,4],[13,9,14],[5,6,0],[1,7,13],[10,7,5],[8,3,2],[14,15,13],[0,12,5],[9,6,13],[12,9,6],[14,0,7],[3,5,2],[4,7,12],[8,5,4],[2,10,7],[2,1,12],[0,2,4],[9,5,10],[0,10,8],[10,11,4],[9,4,14],[0,3,13],[0,3,9],[4,0,11],[11,2,4],[2,7,5],[4,2,0],[0,11,10],[9,7,3],[4,2,12],[4,12,9],[8,2,14],[15,4,2],[14,2,15],[6,8,12],[2,9,4],[6,5,4],[12,10,14],[15,8,0],[5,14,4],[13,14,3],[14,11,15],[14,1,4],[15,11,2],[5,6,14],[13,3,5],[14,3,11],[12,6,9],[0,13,4],[0,12,9],[7,9,1],[7,9,4],[11,14,4],[10,4,11],[9,0,8],[9,0,14],[3,10,14],[12,5,13],[9,8,6],[13,15,10],[6,12,15],[0,9,8],[12,0,11],[3,9,7],[4,6,2],[12,7,9],[14,15,1],[14,13,1],[1,5,12],[5,15,6],[7,11,5],[10,15,12],[1,2,3],[6,5,9],[6,14,8],[5,3,13],[5,14,9],[2,15,13],[6,5,7],[15,14,12],[15,0,9],[10,12,0],[15,0,10],[10,5,3],[12,8,3],[15,2,1],[14,8,2]],[[3,8,0],[5,15,2],[0,8,5],[5,2,11],[9,3,12],[3,12,7],[3,12,15],[11,1,5],[15,12,4],[11,7,2],[5,10,0],[12,7,0],[2,15,4],[6,2,14],[4,9,12],[10,6,12],[8,13,7],[1,13,6],[10,4,14],[6,10,0],[7,8,9],[0,10,13],[3,7,8],[5,15,3],[7,14,1],[1,8,3],[3,13,1],[15,7,8],[8,14,3],[7,0,6],[8,5,0],[5,3,10],[15,4,14],[10,4,1],[13,4,3],[6,12,10],[1,5,3],[11,3,12],[4,7,14],[4,14,10],[14,5,11],[9,1,0],[7,12,3],[11,0,7],[4,9,7],[4,12,14],[15,1,6],[5,7,0],[12,0,8],[3,11,12],[2,1,15],[1,8,3],[10,6,2],[9,8,11],[14,9,11],[12,9,10],[7,12,11],[14,12,10],[11,2,0],[10,14,7],[6,4,0],[12,1,4],[4,7,8],[6,0,13],[7,1,5],[11,12,6],[3,6,10],[15,12,0],[12,11,0],[10,2,9],[1,3,8],[11,1,3],[2,3,12],[13,8,9],[12,9,4],[5,14,13],[7,15,1],[1,11,10],[11,9,15],[15,5,13],[6,3,13],[3,0,4],[0,1,14],[14,2,11],[11,15,5],[0,10,3],[11,12,0],[8,6,14],[11,2,12],[12,7,5],[12,0,8],[5,13,9],[3,13,9],[6,0,12],[4,1,0],[7,14,2],[3,10,0],[1,7,10],[4,2,3],[15,3,1],[2,10,7],[4,9,1],[1,8,7],[1,2,5],[4,15,11],[8,7,11],[14,11,5],[15,10,14],[7,10,12],[9,14,1],[11,9,13],[11,0,7],[2,0,14],[2,15,0],[14,15,5],[6,2,13],[2,9,6],[0,14,6],[3,13,15],[9,11,3],[1,2,12],[3,0,14],[3,9,6],[9,10,4],[6,10,3],[15,8,4],[13,7,0],[10,5,1]],[[0,5,4],[9,10,11],[0,12,11],[15,2,12],[5,9,6],[14,5,11],[9,3,14],[1,8,3],[0,7,12],[2,14,9],[6,11,1],[11,9,4],[11,1,5],[2,3,13],[10,13,14],[2,5,12],[1,9,7],[14,0,10],[4,13,15],[6,7,0],[7,9,6],[4,2,10],[11,14,12],[1,10,9],[7,14,0],[10,4,7],[7,6,4],[15,10,1],[5,13,2],[6,1,9],[3,11,0],[0,1,4],[0,15,13],[5,6,14],[8,1,9],[8,0,11],[12,9,7],[14,1,8],[9,14,4],[0,2,7],[0,7,5],[2,7,1],[14,11,3],[12,3,15],[9,12,4],[9,7,6],[14,8,6],[11,7,15],[9,8,11],[0,15,7],[4,5,3],[1,11,3],[3,14,5],[2,0,8],[6,1,9],[4,10,11],[3,0,9],[10,1,5],[5,15,14],[8,13,0],[14,3,6],[2,5,13],[0,8,14],[12,10,2],[15,2,9],[8,11,10],[4,6,0],[9,5,1],[15,7,11],[15,11,4],[8,13,15],[5,1,9],[6,8,9],[11,13,5],[15,5,7],[6,2,14],[0,15,13],[6,1,10],[4,8,15],[8,5,6],[14,5,1],[1,5,13],[11,7,3],[2,0,12],[10,6,14],[12,11,13],[3,4,11],[7,1,5],[8,7,2],[0,11,12],[10,7,2],[3,11,13],[1,13,11],[0,7,12],[10,11,8],[13,6,2],[13,6,12],[13,5,6],[9,3,8],[15,10,1],[6,11,4],[2,15,0],[3,14,11],[10,3,0],[12,6,15],[8,5,11],[3,4,5],[4,0,2],[7,15,4],[5,8,14],[7,11,3],[12,0,8],[14,6,4],[9,5,4],[9,13,5],[3,5,14],[7,15,11],[2,5,3],[13,15,3],[8,13,14],[15,8,7],[4,5,10],[1,7,9],[13,1,8],[3,6,4],[1,9,7],[15,0,3],[7,12,4]],[[14,12,1],[8,7,14],[15,8,5],[2,7,11],[8,15,14],[3,9,2],[10,15,5],[4,3,1],[3,9,7],[4,1,3],[9,3,13],[10,3,7],[2,3,12],[9,7,0],[9,7,2],[2,5,8],[7,8,4],[14,8,9],[4,13,10],[9,12,14],[5,0,7],[13,9,6],[11,15,12],[15,12,9],[15,8,3],[11,8,5],[9,14,4],[13,1,4],[8,13,11],[1,0,3],[4,2,15],[12,1,4],[14,0,4],[12,4,13],[5,4,3],[3,4,7],[6,13,9],[10,11,1],[11,13,5],[12,1,6],[5,4,0],[12,1,5],[6,15,0],[4,3,14],[10,0,11],[6,0,3],[1,0,5],[5,3,2],[0,7,15],[5,11,1],[8,10,14],[7,1,10],[12,8,11],[4,15,1],[9,12,3],[12,14,15],[13,5,4],[15,13,11],[10,7,3],[12,6,1],[15,8,2],[2,7,13],[15,1,5],[14,7,0],[10,1,4],[10,6,9],[7,15,6],[10,3,11],[11,1,5],[12,1,5],[1,12,8],[6,2,9],[4,7,11],[10,0,6],[0,15,7],[0,7,1],[15,6,4],[4,10,7],[12,14,11],[12,6,14],[1,2,14],[15,9,7],[5,11,3],[11,5,4],[3,5,9],[11,7,9],[12,14,2],[7,12,4],[6,7,13],[0,15,6],[2,7,5],[9,1,14],[15,10,2],[9,8,13],[9,8,2],[9,11,14],[13,15,1],[13,12,14],[14,15,10],[13,11,7],[12,8,5],[3,15,7],[13,10,14],[11,2,5],[0,13,14],[8,15,5],[2,0,11],[10,3,5],[13,12,8],[8,6,4],[8,14,2],[13,6,7],[6,13,15],[7,9,13],[8,5,10],[6,0,7],[14,13,8],[14,2,6],[2,1,10],[7,4,9],[8,6,5],[14,1,13],[1,10,3],[4,0,11],[7,1,2],[1,10,2],[8,5,14],[14,3,11]],[[15,3,6],[12,3,2],[4,2,0],[3,1,6],[2,5,11],[4,8,14],[10,1,8],[10,11,2],[3,5,12],[10,3,4],[13,0,10],[6,1,13],[10,8,5],[9,14,0],[9,0,10],[11,6,4],[0,11,4],[7,14,10],[15,9,14],[10,2,12],[5,6,12],[6,15,11],[7,11,13],[5,10,7],[6,10,0],[7,9,4],[14,9,3],[4,0,11],[9,1,14],[6,8,14],[4,2,11],[0,13,1],[14,13,9],[13,3,6],[10,8,14],[4,12,8],[3,10,6],[5,12,0],[1,6,7],[1,11,10],[0,3,2],[4,12,2],[15,13,9],[11,15,3],[15,3,4],[5,2,9],[12,10,1],[2,15,12],[6,15,0],[7,5,0],[2,12,5],[7,10,8],[0,4,11],[2,1,9],[1,12,13],[15,7,14],[11,12,10],[14,10,4],[3,0,15],[4,15,3],[0,11,15],[13,9,0],[15,6,14],[9,5,12],[7,3,15],[6,3,2],[2,3,8],[7,12,3],[4,8,14],[6,5,15],[1,8,10],[11,10,0],[2,5,14],[11,7,6],[7,10,6],[11,15,1],[8,9,11],[10,3,9],[0,12,11],[13,2,11],[1,2,4],[8,12,5],[6,11,13],[10,4,5],[14,9,8],[3,9,10],[3,2,4],[8,2,15],[7,11,4],[4,11,8],[11,3,12],[3,1,13],[9,5,7],[3,7,9],[14,1,0],[13,10,6],[12,7,6],[11,7,4],[13,14,5],[5,11,0],[15,12,4],[11,14,7],[11,8,5],[9,1,6],[6,9,15],[5,7,3],[8,11,7],[14,15,10],[9,2,15],[11,10,6],[1,6,0],[10,8,1],[7,10,13],[4,13,12],[13,6,7],[10,1,9],[10,9,11],[4,13,8],[14,12,13],[1,12,7],[11,13,5],[11,9,8],[15,1,2],[6,2,14],[9,8,7],[3,5,7],[14,5,8],[4,8,14]],[[2,1,6],[13,10,5],[6,5,14],[7,1,13],[2,12,8],[1,2,7],[9,6,11],[3,1,0],[14,8,1],[6,2,3],[5,6,1],[10,11,1],[14,7,4],[11,15,13],[7,10,1],[2,7,5],[14,1,2],[5,1,13],[7,12,2],[0,7,3],[11,3,5],[3,14,8],[10,2,15],[2,6,11],[8,2,7],[10,5,1],[11,4,13],[4,10,8],[4,13,6],[4,12,14],[4,2,7],[11,13,10],[13,2,9],[6,2,11],[2,15,6],[4,10,1],[0,5,7],[7,14,6],[9,11,7],[11,10,7],[13,11,15],[0,12,6],[10,12,3],[1,2,11],[1,2,13],[7,2,1],[13,5,2],[6,13,4],[13,6,3],[10,11,13],[11,9,4],[8,7,3],[9,14,13],[2,6,3],[9,5,0],[2,3,12],[0,4,8],[5,1,2],[1,6,0],[15,13,0],[4,3,6],[13,11,5],[4,12,1],[7,13,10],[15,4,14],[1,12,10],[1,3,2],[14,6,3],[3,9,0],[6,3,10],[11,12,4],[4,6,15],[2,6,3],[14,3,5],[0,9,13],[4,7,3],[3,10,15],[7,14,2],[3,8,9],[1,9,13],[13,3,4],[13,11,10],[2,12,13],[12,11,7],[9,12,13],[8,15,7],[12,2,14],[10,13,9],[6,13,10],[8,7,13],[6,5,11],[15,5,12],[13,14,4],[4,2,3],[3,5,10],[3,14,13],[5,12,14],[0,13,5],[7,3,8],[14,3,15],[13,8,3],[1,6,5],[4,0,9],[14,5,8],[11,6,5],[3,7,14],[4,13,12],[10,9,13],[0,5,7],[3,6,13],[2,3,14],[4,10,7],[0,5,9],[10,0,11],[11,1,5],[14,1,8],[3,0,8],[9,15,1],[13,7,3],[3,10,14],[8,6,7],[10,5,3],[3,8,14],[13,9,3],[15,9,2],[11,3,0],[14,0,4],[1,12,2]],[[10,14,3],[3,1,0],[6,14,13],[13,11,12],[0,11,8],[8,15,1],[1,14,7],[15,7,13],[15,4,11],[7,5,9],[12,10,5],[1,13,3],[13,0,7],[10,13,15],[11,15,7],[0,11,13],[4,5,0],[10,6,14],[9,13,1],[5,12,8],[9,15,6],[12,11,9],[15,8,6],[4,0,6],[7,8,3],[3,15,0],[0,11,14],[2,7,11],[3,5,4],[10,11,5],[4,2,3],[14,2,10],[3,14,4],[14,5,6],[11,13,4],[12,11,9],[2,8,6],[10,5,6],[6,14,2],[12,15,8],[5,10,2],[6,0,13],[10,14,0],[8,9,10],[8,14,11],[3,10,13],[9,6,8],[0,2,9],[1,15,11],[11,15,9],[10,14,6],[4,15,2],[6,0,3],[7,14,1],[10,0,6],[11,10,9],[11,12,1],[12,5,1],[8,2,4],[11,12,8],[12,14,11],[15,6,1],[14,2,8],[13,0,15],[12,11,14],[10,11,14],[8,3,12],[13,3,6],[6,3,9],[15,0,12],[15,10,14],[10,5,8],[12,15,7],[11,3,5],[15,14,11],[3,6,15],[8,13,9],[2,6,11],[1,12,2],[5,15,8],[2,13,12],[3,13,5],[8,10,14],[11,5,2],[15,6,9],[8,1,0],[6,9,8],[4,9,13],[4,3,6],[0,12,9],[1,13,8],[0,1,4],[2,10,15],[2,14,5],[5,11,1],[13,2,11],[12,2,7],[2,1,5],[11,5,12],[6,10,12],[9,12,0],[11,3,13],[1,13,3],[7,12,14],[5,3,2],[5,0,9],[6,7,3],[2,10,14],[1,11,13],[13,5,4],[5,0,9],[0,7,8],[4,13,14],[10,2,0],[4,11,7],[1,15,12],[4,0,15],[8,10,3],[9,0,5],[2,1,8],[11,0,2],[12,10,15],[4,0,5],[2,9,12],[12,0,5],[1,15,12],[7,9,12],[4,2,14]],[[11,10,12],[0,9,15],[15,7,14],[14,12,2],[13,8,14],[1,13,6],[13,9,15],[7,14,2],[9,11,15],[10,7,0],[2,3,15],[14,7,12],[2,13,11],[15,1,8],[6,9,2],[2,7,14],[9,3,6],[7,6,3],[14,10,9],[10,15,6],[5,1,2],[6,13,9],[14,12,8],[0,13,10],[11,6,15],[3,9,12],[5,0,2],[8,6,14],[7,3,8],[9,12,4],[0,15,5],[9,14,4],[7,3,2],[3,6,8],[0,2,5],[14,13,11],[5,3,7],[7,6,1],[1,15,7],[6,5,15],[3,10,14],[8,13,15],[1,11,15],[8,14,10],[4,10,2],[11,9,12],[15,7,6],[6,7,13],[13,0,10],[15,7,12],[15,5,2],[1,0,11],[5,8,15],[5,7,12],[8,0,11],[13,11,5],[1,2,10],[7,13,11],[1,3,6],[15,3,2],[2,5,6],[2,6,14],[12,8,0],[1,7,9],[1,4,6],[14,1,6],[5,6,0],[11,13,9],[5,11,13],[4,8,6],[7,2,1],[6,9,10],[5,7,11],[2,5,0],[11,14,5],[14,9,1],[12,0,7],[10,12,15],[11,9,10],[9,7,0],[4,13,1],[15,1,12],[2,8,12],[0,14,2],[12,13,9],[5,8,3],[14,2,15],[7,0,6],[13,0,11],[1,14,12],[8,2,4],[6,0,13],[3,5,8],[13,8,7],[1,2,12],[13,11,1],[3,7,13],[15,1,12],[7,5,4],[13,0,15],[10,13,2],[1,13,15],[8,11,15],[8,12,13],[13,1,5],[13,14,4],[15,7,10],[7,2,0],[10,11,15],[0,2,3],[8,1,3],[14,9,4],[13,5,4],[15,10,8],[1,15,12],[8,0,12],[1,10,2],[3,6,10],[12,13,3],[3,9,5],[15,11,2],[9,15,10],[9,3,0],[4,10,2],[0,5,3],[6,10,15],[15,9,6],[13,4,9]],[[0,10,12],[8,5,6],[4,0,14],[14,12,11],[3,0,14],[8,1,14],[9,10,6],[9,10,5],[4,0,1],[1,12,14],[11,9,4],[6,2,10],[12,4,5],[2,0,3],[15,3,8],[11,5,3],[11,10,1],[10,4,5],[14,9,11],[7,0,2],[0,9,1],[9,5,7],[9,0,3],[1,15,7],[8,3,9],[9,4,7],[9,12,13],[12,8,1],[10,8,14],[6,14,12],[4,3,14],[13,6,14],[8,10,1],[12,0,1],[8,1,10],[6,3,15],[14,1,6],[2,5,9],[11,3,7],[4,5,8],[3,0,2],[15,6,3],[2,6,8],[2,5,8],[7,2,10],[7,15,5],[2,10,8],[0,7,5],[12,6,10],[0,2,7],[7,13,8],[12,10,0],[4,6,3],[8,14,12],[1,15,10],[6,7,9],[8,5,7],[12,14,3],[3,8,9],[14,9,13],[4,5,1],[10,4,8],[8,2,10],[3,1,9],[12,3,14],[4,11,8],[5,15,14],[5,3,2],[5,6,7],[8,9,3],[15,7,14],[3,7,15],[10,6,5],[10,4,11],[9,7,12],[13,15,0],[8,13,4],[12,1,7],[4,12,1],[5,15,6],[4,13,11],[0,5,4],[14,11,2],[4,6,3],[8,9,6],[8,6,5],[11,0,4],[0,13,4],[3,6,5],[5,1,13],[13,12,7],[0,6,4],[13,0,3],[11,8,7],[12,5,0],[10,14,3],[7,5,10],[5,6,2],[6,3,9],[9,11,1],[1,14,12],[3,13,2],[3,5,6],[6,3,12],[13,14,8],[11,5,4],[3,12,11],[12,8,14],[15,3,9],[14,5,11],[3,11,4],[7,12,5],[1,15,9],[14,5,9],[6,9,14],[9,14,7],[7,11,2],[6,7,13],[10,11,0],[5,1,12],[9,1,5],[9,7,10],[2,15,9],[9,12,13],[5,7,6],[11,3,1],[3,7,5],[15,10,5]],[[7,8,1],[3,6,13],[11,2,4],[1,13,6],[2,1,13],[0,9,12],[11,8,3],[6,10,4],[6,9,15],[15,7,13],[15,5,4],[11,3,13],[15,14,8],[13,15,5],[9,5,14],[14,8,9],[0,4,1],[4,14,9],[13,11,3],[3,8,9],[0,5,4],[2,3,9],[3,12,5],[15,1,5],[9,2,5],[7,0,4],[2,7,8],[15,9,7],[11,7,15],[12,0,9],[9,13,5],[9,2,7],[0,13,5],[14,6,3],[12,14,4],[13,2,15],[3,10,12],[4,9,7],[5,11,0],[11,12,14],[7,6,5],[10,12,5],[13,10,6],[0,11,2],[7,12,15],[0,9,6],[1,15,6],[5,4,3],[3,0,6],[4,2,15],[7,8,14],[12,11,1],[9,6,4],[8,5,1],[1,3,6],[10,8,1],[6,8,5],[5,10,3],[11,13,0],[8,0,12],[9,6,5],[14,11,8],[11,14,3],[2,15,3],[13,10,14],[10,3,4],[10,8,7],[12,8,2],[8,4,10],[1,14,7],[12,10,8],[4,14,13],[9,14,5],[7,2,15],[13,6,11],[8,5,10],[13,2,5],[15,10,2],[14,5,6],[8,4,12],[11,15,0],[11,3,15],[13,9,0],[5,9,14],[4,15,8],[2,9,11],[10,5,1],[7,14,1],[9,4,3],[14,15,8],[13,12,3],[8,7,12],[1,8,10],[9,4,5],[2,13,4],[6,10,3],[10,13,4],[15,4,0],[12,11,5],[6,13,4],[0,3,5],[5,13,15],[13,6,2],[5,7,14],[0,12,14],[1,14,11],[6,9,7],[8,13,7],[13,4,14],[3,7,13],[13,12,9],[3,10,1],[3,0,11],[14,10,12],[15,6,10],[13,2,8],[7,4,14],[13,2,0],[6,1,11],[9,8,0],[3,1,0],[4,13,9],[15,13,8],[11,9,8],[0,12,8],[7,4,3],[13,3,7],[3,11,12]],[[15,14,7],[11,6,0],[12,14,8],[6,15,3],[2,5,10],[5,1,10],[15,2,7],[10,12,9],[10,13,9],[14,2,8],[1,6,8],[9,6,13],[1,13,11],[0,10,5],[7,11,14],[14,10,1],[10,3,2],[15,0,5],[13,8,14],[15,8,9],[11,14,12],[7,9,14],[1,14,3],[7,6,0],[11,10,9],[10,4,0],[5,6,11],[14,0,11],[8,14,10],[15,1,2],[13,2,10],[2,12,7],[2,5,10],[11,15,14],[5,1,15],[13,9,15],[8,10,12],[10,0,8],[2,7,0],[4,12,0],[7,8,14],[9,3,13],[11,13,1],[12,6,11],[2,4,14],[0,2,10],[9,10,8],[9,6,7],[13,3,10],[12,4,7],[13,8,2],[12,15,13],[6,10,15],[13,6,7],[4,15,12],[4,2,6],[5,14,2],[15,1,6],[12,10,1],[1,14,7],[11,15,0],[10,14,1],[14,5,3],[1,7,10],[8,10,0],[15,6,8],[15,3,2],[6,10,1],[11,2,12],[12,3,10],[1,11,15],[9,0,8],[1,7,11],[5,14,3],[2,3,0],[7,15,8],[14,9,12],[14,5,1],[0,4,14],[1,3,9],[10,11,0],[0,13,15],[15,4,11],[8,14,0],[10,14,3],[11,2,13],[11,13,4],[0,9,15],[4,12,14],[10,9,14],[3,14,13],[6,8,11],[7,3,0],[10,3,5],[6,14,1],[6,0,8],[13,2,1],[10,8,15],[7,4,13],[4,7,3],[9,7,5],[14,12,9],[5,10,11],[14,4,1],[2,4,5],[15,7,14],[14,11,9],[1,8,15],[11,5,13],[15,4,8],[10,1,12],[6,14,2],[11,7,10],[4,11,14],[2,0,4],[10,14,1],[10,9,11],[6,15,4],[10,12,15],[3,4,15],[15,1,7],[0,8,2],[10,13,6],[13,9,4],[2,12,1],[9,12,2],[13,2,8],[9,12,13]],[[13,0,3],[13,3,10],[3,6,14],[6,7,14],[8,15,12],[9,7,13],[4,6,14],[13,5,15],[12,13,6],[0,9,12],[1,10,14],[13,11,12],[11,3,9],[5,0,7],[4,5,0],[11,0,8],[5,4,11],[15,4,14],[9,10,14],[12,13,6],[14,13,3],[11,6,13],[6,1,3],[15,7,1],[11,3,9],[7,2,1],[0,11,15],[12,10,9],[5,13,1],[4,2,0],[9,1,12],[8,12,11],[15,4,10],[13,11,12],[5,10,0],[11,0,15],[6,1,10],[15,10,7],[11,10,8],[2,6,3],[7,12,15],[6,13,12],[1,6,4],[0,8,4],[8,9,7],[1,5,12],[1,15,8],[5,10,13],[14,9,0],[6,0,12],[12,11,15],[4,3,13],[5,0,4],[3,13,14],[12,4,6],[6,10,0],[14,0,4],[11,13,9],[2,12,5],[11,13,4],[12,0,7],[5,1,14],[12,11,10],[6,15,8],[12,13,4],[15,10,14],[8,5,11],[15,1,0],[12,5,1],[8,4,11],[11,0,7],[14,2,10],[3,0,11],[15,2,3],[1,9,7],[9,13,11],[0,10,11],[10,5,8],[5,9,15],[5,14,0],[2,15,3],[8,0,11],[15,14,7],[13,7,5],[2,8,15],[13,2,15],[13,5,14],[12,11,2],[0,4,13],[3,12,5],[5,12,0],[7,3,15],[0,12,3],[1,11,2],[2,7,1],[0,5,14],[9,1,7],[9,13,3],[1,0,9],[2,8,14],[8,1,9],[12,10,14],[6,1,11],[12,15,4],[7,11,6],[9,13,6],[10,7,6],[13,7,6],[6,10,11],[14,7,13],[8,9,13],[3,4,11],[6,5,10],[0,10,2],[1,4,0],[6,14,15],[3,7,1],[1,6,8],[8,12,9],[12,2,15],[9,7,2],[8,12,7],[14,4,3],[12,9,4],[9,12,4],[13,5,0],[10,12,1],[12,5,11]]]
ZW = 401
def setup_inputs(rng):
    return {"z": rng.standard_normal((N, 128, ZW), dtype=np.float32), "g": rng.random((N, 128, T * K), dtype=np.float32)}
def reference(z, g):
    y = np.zeros((N, 128, T), np.float64)
    fill = [0] * N
    for r in range(N):
        for t in range(T):
            for k, e in enumerate(ROUTE[r][t]):
                y[r][:, t] += g[r][:, t * K + k].astype(np.float64) * z[e][:, fill[e]].astype(np.float64)
                fill[e] += 1
    return {"y": y.astype(z.dtype)}

@@ -1,0 +1,212 @@
+from concourse.bass import DstId, RemoteDMATransfer
+from concourse.mybir import AluOpType
+
+WD = 90
+NP = 48
+SCRATCH = {
+    "zs": ("sbuf", [128, 401], "float32"),
+    "zh": ("sbuf", [128, WD], "float32"),
+    "zland": ("sbuf", [128, 384], "float32"),
+    "gs": ("sbuf", [128, 384], "float32"),
+    "pb": ("sbuf", [128, 8, 3 * NP], "bfloat16"),
+    "pf": ("sbuf", [128, 3, 384], "float32"),
+    "ia": ("sbuf", [128, 129], "float32"),
+    "idr": ("dram", [129, 128], "float32"),
+    "ident": ("sbuf", [128, 128], "float32"),
+    "ib": ("sbuf", [128, 129], "bfloat16"),
+    "ibr": ("dram", [129, 128], "bfloat16"),
+    "dmat": ("sbuf", [128, 128], "bfloat16"),
+    "zt": ("sbuf", [128, 3, 128], "float32"),
+    "p0": ("sbuf", [128, 128], "float32"),
+    "p2": ("sbuf", [128, 128], "float32"),
+    "ys": ("sbuf", [128, 128], "float32"),
+    "pst0": ("psum", [128, 512], "float32"),
+    "pst1": ("psum", [128, 512], "float32"),
+    "pst2": ("psum", [128, 512], "float32"),
+    "psz": ("psum", [128, 512], "float32"),
+    "psa": ("psum", [128, 512], "float32"),
+    "psp0": ("psum", [128, 512], "float32"),
+    "psp1": ("psum", [128, 512], "float32"),
+    "psp2": ("psum", [128, 512], "float32"),
+}
+SEMAPHORES = ["zld", "gld", "zarr", "sent", "arr0", "arr1", "arr2", "pbs", "parr", "pfr", "ias", "id1", "id2",
+              "tp", "tc", "mm", "dv", "yst", "ibs", "ib1", "ib2", "pm0", "pm1", "pm2"]
+
+CROSS = [2, 3, 6, 7]
+SAME = [0, 1, 4, 5]
+PLAN = {}
+
+
+def plan(T):
+    if "ok" in PLAN:
+        return PLAN
+    route = T.tables["ROUTE"]
+    n = len(route)
+    nt = T.tables["T"]
+    cnt = [[0] * n for _ in range(n)]
+    for r in range(n):
+        for t in range(nt):
+            for e in route[r][t]:
+                cnt[e][r] += 1
+    off = [[0] * n for _ in range(n)]
+    for e in range(n):
+        s = 0
+        for r in range(n):
+            off[e][r] = s
+            s += cnt[e][r]
+    serve = [[[] for _ in range(8)] for _ in range(n)]
+    for e in range(n):
+        par = e & 1
+        rot = (e // 2) % 4
+        for q in range(4):
+            serve[e][CROSS[(q + rot) % 4]] = [1 - par + 4 * q, 1 - par + 4 * q + 2]
+            serve[e][SAME[(q + rot) % 4]] = [d for d in (par + 4 * q, par + 4 * q + 2) if d != e]
+    land = [[0] * n for _ in range(n)]
+    group = [[0] * n for _ in range(n)]
+    for r in range(n):
+        keys = []
+        for e in range(n):
+            if e == r:
+                keys.append((-1.0, e))
+                continue
+            k = [c for c in range(8) if r in serve[e][c]][0]
+            key = 0.0 if k == e % 8 else 2.0
+            key += 0.7 * serve[e][k].index(r)
+            if (e & 1) != (r & 1) and (e ^ 1) != r:
+                key += 0.5
+            keys.append((key, e))
+        s = 0
+        for _, e in sorted(keys):
+            land[r][e] = s
+            group[r][e] = s // 128
+            s += cnt[e][r]
+    idx = [[[0] * 3 for _ in range(nt)] for _ in range(n)]
+    for r in range(n):
+        fill = [0] * n
+        for t in range(nt):
+            for k, e in enumerate(route[r][t]):
+                idx[r][t][k] = land[r][e] + fill[e]
+                fill[e] += 1
+    PLAN.update(cnt=cnt, off=off, serve=serve, land=land, group=group, idx=idx, n=n, nt=nt, ok=True)
+    return PLAN
+
+
+def rank_program(g, core, T, topo):
+    P = plan(T)
+    chip, k = core // 8, core % 8
+    e = chip
+    rcore = T.cores[e]
+    is_rank = core == rcore
+    cnt, off, serve, land, group, idx = P["cnt"], P["off"], P["serve"], P["land"], P["group"], P["idx"]
+    S = T.sem
+    V = g.vector
+    nt = P["nt"]
+
+    if is_rank:
+        g.sync.dma_start(T.zs[:], T.z[:]).then_inc(S.zld, 16)
+        a = off[e][e]
+        g.scalar.dma_start(T.zland[:, land[e][e]:land[e][e] + cnt[e][e]], T.z[:, a:a + cnt[e][e]]).then_inc(
+            S["arr%d" % group[e][e]], 16)
+        g.scalar.dma_start(T.gs[:], T.g[:]).then_inc(S.gld, 16)
+        V.memset(T.ia[:], 0.0).then_inc(S.ias, 1)
+        V.memset(T.ib[:], 0.0).then_inc(S.ibs, 1)
+        V.wait_ge(S.ias, 1)
+        V.memset(T.ia[:, 0:1], 1.0).then_inc(S.ias, 1)
+        V.wait_ge(S.ibs, 1)
+        V.memset(T.ib[:, 0:1], 1.0).then_inc(S.ibs, 1)
+        V.memset(T.ib[:, 128:129], -1.0).then_inc(S.ibs, 1)
+        g.sync.wait_ge(S.ias, 2)
+        g.sync.dma_start(T.idr[:], T.ia[:]).then_inc(S.id1, 16)
+        g.sync.wait_ge(S.id1, 16)
+        g.sync.dma_start(T.ident[:], T.idr[0:128, :]).then_inc(S.id2, 16)
+        g.scalar.wait_ge(S.ibs, 3)
+        g.scalar.dma_start(T.ibr[:], T.ib[:]).then_inc(S.ib1, 16)
+        g.scalar.wait_ge(S.ib1, 16)
+        g.scalar.dma_start(T.dmat[:], T.ibr[0:128, :]).then_inc(S.ib2, 16)
+
+    V.memset(T.pb[:, k], 0.0).then_inc(S.pbs, 1)
+    V.wait_ge(S.pbs, 1)
+    for jj in range(NP):
+        j = k * NP + jj
+        c = idx[e][j % nt][j // nt]
+        x = (c // 128) * NP + jj
+        V.memset(T.pb[0:c % 128 + 1, k, x:x + 1], 1.0).then_inc(S.pbs, 1)
+
+    sent = 0
+    if not is_rank:
+        rid, pid, _ = topo.addr(rcore)
+        g.wait_ge(S.pbs, NP + 1)
+        g.remote_dma(T.pb[:, k], T.pb[:, k], S.parr, S.sent, pid, rid, 0xFFFF)
+        sent += 16
+        g.wait_ge(S.zarr, 2)
+    else:
+        g.wait_ge(S.zld, 16)
+        trs = []
+        i = 0
+        for h in range(8):
+            if h == k:
+                continue
+            ds = serve[e][h]
+            ws = min(off[e][ds[0]], 401 - WD)
+            rid, pid, _ = topo.addr(chip * 8 + h)
+            trs.append(RemoteDMATransfer(dst_ids=[DstId(rid=rid, pnc=pid)], dma_engine_mask=3 << (2 * i),
+                                         remote_sem=S.zarr, src=T.zs[:, ws:ws + WD], dst=T.zh[:]))
+            i += 1
+        g.remote_dma_fused(trs, local_sem=S.sent)
+        sent += 14
+
+    ds = serve[e][k]
+    ws = 0 if is_rank else min(off[e][ds[0]], 401 - WD)
+    src = T.zs if is_rank else T.zh
+    for d in ds:
+        a = off[e][d] - ws
+        w = cnt[e][d]
+        rid, pid, _ = topo.addr(T.cores[d])
+        g.remote_dma(T.zland[:, land[d][e]:land[d][e] + w], src[:, a:a + w], S["arr%d" % group[d][e]], S.sent,
+                     pid, rid, 0x00FF)
+        sent += 8
+    g.wait_ge(S.sent, sent)
+    if not is_rank:
+        return
+
+    need = [0, 0, 0]
+    for s in range(P["n"]):
+        need[group[e][s]] += 16 if s == e else 8
+    pst = [T.pst0, T.pst1, T.pst2]
+    psp = [T.psp0, T.psp1, T.psp2]
+    PE = g.tensor
+    PE.wait_ge(S.ib2, 16)
+    PE.wait_ge(S.pbs, NP + 1)
+    PE.wait_ge(S.parr, 7 * 16)
+    for h in range(8):
+        b, i = h // 3, h % 3
+        PE.matmul(psp[b][:, i * 3 * NP:(i + 1) * 3 * NP], T.dmat[:], T.pb[:, h], start=True, stop=True).then_inc(
+            S["pm%d" % b], 1)
+    for h in range(8):
+        b, i = h // 3, h % 3
+        if i == 0:
+            V.wait_ge(S["pm%d" % b], 3 if b < 2 else 2)
+        V.tensor_copy(T.pf[:, :, h * NP:(h + 1) * NP], psp[b][:, i * 3 * NP:(i + 1) * 3 * NP]).then_inc(S.pfr, 1)
+    PE.wait_ge(S.id2, 16)
+    for ch in range(3):
+        PE.wait_ge(S["arr%d" % ch], need[ch])
+        PE.matmul(pst[ch][:, 0:128], T.zland[:, ch * 128:(ch + 1) * 128], T.ident[:], start=True, stop=True).then_inc(
+            S.tp, 1)
+        V.wait_ge(S.tp, ch + 1)
+        V.tensor_copy(T.zt[:, ch], pst[ch][:, 0:128]).then_inc(S.tc, 1)
+        PE.wait_ge(S.tc, ch + 1)
+        if ch == 0:
+            PE.wait_ge(S.pfr, 8)
+        PE.matmul(T.psz[:, 0:384], T.zt[:, ch], T.pf[:, ch], start=(ch == 0), stop=(ch == 2)).then_inc(S.mm, 1)
+    V.wait_ge(S.mm, 3)
+    V.wait_ge(S.gld, 16)
+    V.tensor_tensor(T.p0[:], T.gs[:, 0::3], T.psz[:, 0:128], AluOpType.mult).then_inc(S.dv, 1)
+    V.tensor_tensor(T.psa[:, 0:128], T.gs[:, 1::3], T.psz[:, 128:256], AluOpType.mult).then_inc(S.dv, 1)
+    V.tensor_tensor(T.p2[:], T.gs[:, 2::3], T.psz[:, 256:384], AluOpType.mult).then_inc(S.dv, 1)
+    V.wait_ge(S.dv, 3)
+    V.tensor_tensor(T.psa[:, 128:256], T.p0[:], T.psa[:, 0:128], AluOpType.add).then_inc(S.dv, 1)
+    V.wait_ge(S.dv, 4)
+    V.tensor_tensor(T.ys[:], T.p2[:], T.psa[:, 128:256], AluOpType.add).then_inc(S.dv, 1)
+    g.sync.wait_ge(S.dv, 5)
+    g.sync.dma_start(T.y[:], T.ys[:]).then_inc(S.yst, 16)
+    g.sync.wait_ge(S.yst, 16)

@@ -23,18 +23,44 @@ SCRATCH = {
     "pst0": ("psum", [128, 512], "float32"),
     "pst1": ("psum", [128, 512], "float32"),
     "pst2": ("psum", [128, 512], "float32"),
-    "psz": ("psum", [128, 512], "float32"),
     "psa": ("psum", [128, 512], "float32"),
     "psp0": ("psum", [128, 512], "float32"),
     "psp1": ("psum", [128, 512], "float32"),
     "psp2": ("psum", [128, 512], "float32"),
 }
 SEMAPHORES = ["zld", "gld", "zarr", "sent", "arr0", "arr1", "arr2", "pbs", "parr", "pfr", "ias", "id1", "id2",
-              "tp", "tc", "mm", "dv", "yst", "ibs", "ib1", "ib2", "pm0", "pm1", "pm2"]
+              "tp", "tc", "mk0", "mk1", "mk2", "dv", "yst", "ib2", "pm0", "pm1", "pm2", "go"]
 
 CROSS = [2, 3, 6, 7]
 SAME = [0, 1, 4, 5]
+HALVES = [(0, 1), (0, 2), (0, 3), (1, 2), (1, 3), (2, 3)]
 PLAN = {}
+
+
+def pairs_of(e):
+    par = e & 1
+    cr = [[1 - par + 4 * q, 1 - par + 4 * q + 2] for q in range(4)]
+    sm = [[d for d in (par + 4 * q, par + 4 * q + 2) if d != e] for q in range(4)]
+    return cr, sm
+
+
+def port_cost(ch, cnt, n):
+    sw = {}
+    ml = {}
+    for e in range(n):
+        cr, sm = pairs_of(e)
+        for q in range(4):
+            d = 0 if q in HALVES[ch[e][0]] else 1
+            for r in cr[q]:
+                ml[(e, d)] = ml.get((e, d), 0) + cnt[e][r]
+                if r != e ^ 1:
+                    sw[(0, e ^ 1, d)] = sw.get((0, e ^ 1, d), 0) + cnt[e][r]
+                    sw[(1, r, d)] = sw.get((1, r, d), 0) + cnt[e][r]
+            d = 0 if q in HALVES[ch[e][1]] else 1
+            for r in sm[q]:
+                sw[(0, e, d)] = sw.get((0, e, d), 0) + cnt[e][r]
+                sw[(1, r, d)] = sw.get((1, r, d), 0) + cnt[e][r]
+    return max(sw.values()), sum(x * x for x in sw.values()) + sum(x * x for x in ml.values())
 
 
 def plan(T):
@@ -54,13 +80,28 @@ def plan(T):
         for r in range(n):
             off[e][r] = s
             s += cnt[e][r]
+    ch = []
+    for e in range(n):
+        rot = (e // 2) % 4
+        a = HALVES.index(tuple(sorted(q for q in range(4) if (q + rot) % 4 < 2)))
+        ch.append((a, a))
+    for _ in range(4):
+        for e in range(n):
+            best = None
+            for a in range(6):
+                for b in range(6):
+                    ch[e] = (a, b)
+                    v = port_cost(ch, cnt, n)
+                    if best is None or v < best[0]:
+                        best = (v, (a, b))
+            ch[e] = best[1]
     serve = [[[] for _ in range(8)] for _ in range(n)]
     for e in range(n):
-        par = e & 1
-        rot = (e // 2) % 4
-        for q in range(4):
-            serve[e][CROSS[(q + rot) % 4]] = [1 - par + 4 * q, 1 - par + 4 * q + 2]
-            serve[e][SAME[(q + rot) % 4]] = [d for d in (par + 4 * q, par + 4 * q + 2) if d != e]
+        cr, sm = pairs_of(e)
+        for prs, cores, half in ((cr, CROSS, HALVES[ch[e][0]]), (sm, SAME, HALVES[ch[e][1]])):
+            order = [q for q in range(4) if q in half] + [q for q in range(4) if q not in half]
+            for i, q in enumerate(order):
+                serve[e][cores[i]] = prs[q]
     land = [[0] * n for _ in range(n)]
     group = [[0] * n for _ in range(n)]
     for r in range(n):
@@ -70,7 +111,7 @@ def plan(T):
                 keys.append((-1.0, e))
                 continue
             k = [c for c in range(8) if r in serve[e][c]][0]
-            key = 0.0 if k == e % 8 else 2.0
+            key = 0.0 if k == e % 8 else (1.2 if k in CROSS else 2.0)
             key += 0.7 * serve[e][k].index(r)
             if (e & 1) != (r & 1) and (e ^ 1) != r:
                 key += 0.5
@@ -101,28 +142,23 @@ def rank_program(g, core, T, topo):
     S = T.sem
     V = g.vector
     nt = P["nt"]
+    role = (k - rcore % 8) % 8
+    rrid, rpid, _ = topo.addr(rcore)
 
     if is_rank:
         g.sync.dma_start(T.zs[:], T.z[:]).then_inc(S.zld, 16)
         a = off[e][e]
         g.scalar.dma_start(T.zland[:, land[e][e]:land[e][e] + cnt[e][e]], T.z[:, a:a + cnt[e][e]]).then_inc(
             S["arr%d" % group[e][e]], 16)
-        g.scalar.dma_start(T.gs[:], T.g[:]).then_inc(S.gld, 16)
-        V.memset(T.ia[:], 0.0).then_inc(S.ias, 1)
-        V.memset(T.ib[:], 0.0).then_inc(S.ibs, 1)
+    if role in (1, 2):
+        buf, drm = (T.ia, T.idr) if role == 1 else (T.ib, T.ibr)
+        V.memset(buf[:], 0.0).then_inc(S.ias, 1)
         V.wait_ge(S.ias, 1)
-        V.memset(T.ia[:, 0:1], 1.0).then_inc(S.ias, 1)
-        V.wait_ge(S.ibs, 1)
-        V.memset(T.ib[:, 0:1], 1.0).then_inc(S.ibs, 1)
-        V.memset(T.ib[:, 128:129], -1.0).then_inc(S.ibs, 1)
-        g.sync.wait_ge(S.ias, 2)
-        g.sync.dma_start(T.idr[:], T.ia[:]).then_inc(S.id1, 16)
-        g.sync.wait_ge(S.id1, 16)
-        g.sync.dma_start(T.ident[:], T.idr[0:128, :]).then_inc(S.id2, 16)
-        g.scalar.wait_ge(S.ibs, 3)
-        g.scalar.dma_start(T.ibr[:], T.ib[:]).then_inc(S.ib1, 16)
-        g.scalar.wait_ge(S.ib1, 16)
-        g.scalar.dma_start(T.dmat[:], T.ibr[0:128, :]).then_inc(S.ib2, 16)
+        V.memset(buf[:, 0:1], 1.0).then_inc(S.ias, 1)
+        if role == 2:
+            V.memset(buf[:, 128:129], -1.0).then_inc(S.ias, 1)
+        g.sync.wait_ge(S.ias, role + 1)
+        g.sync.dma_start(drm[:], buf[:]).then_inc(S.id1, 16)
 
     V.memset(T.pb[:, k], 0.0).then_inc(S.pbs, 1)
     V.wait_ge(S.pbs, 1)
@@ -134,26 +170,31 @@ def rank_program(g, core, T, topo):
 
     sent = 0
     if not is_rank:
-        rid, pid, _ = topo.addr(rcore)
+        if role == 1:
+            g.wait_ge(S.id1, 16)
+            g.remote_dma(T.ident[:], T.idr[0:128, :], S.id2, S.sent, rpid, rrid, 0xFFFF)
+            sent += 16
+        if role == 2:
+            g.wait_ge(S.id1, 16)
+            g.remote_dma(T.dmat[:], T.ibr[0:128, :], S.ib2, S.sent, rpid, rrid, 0xFFFF)
+            sent += 16
         g.wait_ge(S.pbs, NP + 1)
-        g.remote_dma(T.pb[:, k], T.pb[:, k], S.parr, S.sent, pid, rid, 0xFFFF)
+        g.remote_dma(T.pb[:, k], T.pb[:, k], S.parr, S.sent, rpid, rrid, 0xFFFF)
         sent += 16
-        g.wait_ge(S.zarr, 2)
+        g.wait_ge(S.zarr, 4)
     else:
         g.wait_ge(S.zld, 16)
-        trs = []
-        i = 0
-        for h in range(8):
-            if h == k:
-                continue
-            ds = serve[e][h]
-            ws = min(off[e][ds[0]], 401 - WD)
-            rid, pid, _ = topo.addr(chip * 8 + h)
-            trs.append(RemoteDMATransfer(dst_ids=[DstId(rid=rid, pnc=pid)], dma_engine_mask=3 << (2 * i),
-                                         remote_sem=S.zarr, src=T.zs[:, ws:ws + WD], dst=T.zh[:]))
-            i += 1
-        g.remote_dma_fused(trs, local_sem=S.sent)
-        sent += 14
+        for cores in (CROSS, SAME):
+            trs = []
+            for h in cores:
+                if h == k:
+                    continue
+                ws = min(off[e][serve[e][h][0]], 401 - WD)
+                rid, pid, _ = topo.addr(chip * 8 + h)
+                trs.append(RemoteDMATransfer(dst_ids=[DstId(rid=rid, pnc=pid)], dma_engine_mask=15 << (4 * len(trs)),
+                                             remote_sem=S.zarr, src=T.zs[:, ws:ws + WD], dst=T.zh[:]))
+            g.remote_dma_fused(trs, local_sem=S.sent)
+            sent += 4 * len(trs)
 
     ds = serve[e][k]
     ws = 0 if is_rank else min(off[e][ds[0]], 401 - WD)
@@ -165,6 +206,10 @@ def rank_program(g, core, T, topo):
         g.remote_dma(T.zland[:, land[d][e]:land[d][e] + w], src[:, a:a + w], S["arr%d" % group[d][e]], S.sent,
                      pid, rid, 0x00FF)
         sent += 8
+    if is_rank:
+        g.sem_inc(S.go, 1)
+        g.scalar.wait_ge(S.go, 1)
+        g.scalar.dma_start(T.gs[:], T.g[:]).then_inc(S.gld, 16)
     g.wait_ge(S.sent, sent)
     if not is_rank:
         return
@@ -197,14 +242,18 @@ def rank_program(g, core, T, topo):
         PE.wait_ge(S.tc, ch + 1)
         if ch == 0:
             PE.wait_ge(S.pfr, 8)
-        PE.matmul(T.psz[:, 0:384], T.zt[:, ch], T.pf[:, ch], start=(ch == 0), stop=(ch == 2)).then_inc(S.mm, 1)
-    V.wait_ge(S.mm, 3)
+        for kp in range(3):
+            PE.matmul(psp[kp][:, 0:128], T.zt[:, ch], T.pf[:, ch, kp * 128:(kp + 1) * 128], start=(ch == 0),
+                      stop=(ch == 2)).then_inc(S["mk%d" % kp], 1)
     V.wait_ge(S.gld, 16)
-    V.tensor_tensor(T.p0[:], T.gs[:, 0::3], T.psz[:, 0:128], AluOpType.mult).then_inc(S.dv, 1)
-    V.tensor_tensor(T.psa[:, 0:128], T.gs[:, 1::3], T.psz[:, 128:256], AluOpType.mult).then_inc(S.dv, 1)
-    V.tensor_tensor(T.p2[:], T.gs[:, 2::3], T.psz[:, 256:384], AluOpType.mult).then_inc(S.dv, 1)
-    V.wait_ge(S.dv, 3)
+    V.wait_ge(S.mk0, 3)
+    V.tensor_tensor(T.p0[:], T.gs[:, 0::3], psp[0][:, 0:128], AluOpType.mult).then_inc(S.dv, 1)
+    V.wait_ge(S.mk1, 3)
+    V.tensor_tensor(T.psa[:, 0:128], T.gs[:, 1::3], psp[1][:, 0:128], AluOpType.mult).then_inc(S.dv, 1)
+    V.wait_ge(S.dv, 2)
     V.tensor_tensor(T.psa[:, 128:256], T.p0[:], T.psa[:, 0:128], AluOpType.add).then_inc(S.dv, 1)
+    V.wait_ge(S.mk2, 3)
+    V.tensor_tensor(T.p2[:], T.gs[:, 2::3], psp[2][:, 0:128], AluOpType.mult).then_inc(S.dv, 1)
     V.wait_ge(S.dv, 4)
     V.tensor_tensor(T.ys[:], T.p2[:], T.psa[:, 128:256], AluOpType.add).then_inc(S.dv, 1)
     g.sync.wait_ge(S.dv, 5)

from concourse.bass import DstId, RemoteDMATransfer
from concourse.mybir import AluOpType

WD = 90
NP = 48
SCRATCH = {
    "zs": ("sbuf", [128, 401], "float32"),
    "zh": ("sbuf", [128, WD], "float32"),
    "zland": ("sbuf", [128, 384], "float32"),
    "gs": ("sbuf", [128, 384], "float32"),
    "pb": ("sbuf", [128, 8, 3 * NP], "bfloat16"),
    "pf": ("sbuf", [128, 3, 384], "float32"),
    "ia": ("sbuf", [128, 129], "float32"),
    "idr": ("dram", [129, 128], "float32"),
    "ident": ("sbuf", [128, 128], "float32"),
    "ib": ("sbuf", [128, 129], "bfloat16"),
    "ibr": ("dram", [129, 128], "bfloat16"),
    "dmat": ("sbuf", [128, 128], "bfloat16"),
    "zt": ("sbuf", [128, 3, 128], "float32"),
    "p0": ("sbuf", [128, 128], "float32"),
    "p2": ("sbuf", [128, 128], "float32"),
    "ys": ("sbuf", [128, 128], "float32"),
    "pst0": ("psum", [128, 512], "float32"),
    "pst1": ("psum", [128, 512], "float32"),
    "pst2": ("psum", [128, 512], "float32"),
    "psa": ("psum", [128, 512], "float32"),
    "psp0": ("psum", [128, 512], "float32"),
    "psp1": ("psum", [128, 512], "float32"),
    "psp2": ("psum", [128, 512], "float32"),
}
SEMAPHORES = ["zld", "gld", "zarr", "sent", "arr0", "arr1", "arr2", "pbs", "parr", "pfr", "ias", "id1", "id2",
              "tp", "tc", "mk0", "mk1", "mk2", "dv", "yst", "ib2", "pm0", "pm1", "pm2", "go"]

CROSS = [2, 3, 6, 7]
SAME = [0, 1, 4, 5]
HALVES = [(0, 1), (0, 2), (0, 3), (1, 2), (1, 3), (2, 3)]
PLAN = {}


def pairs_of(e):
    par = e & 1
    cr = [[1 - par + 4 * q, 1 - par + 4 * q + 2] for q in range(4)]
    sm = [[d for d in (par + 4 * q, par + 4 * q + 2) if d != e] for q in range(4)]
    return cr, sm


def port_cost(ch, cnt, n):
    sw = {}
    ml = {}
    for e in range(n):
        cr, sm = pairs_of(e)
        for q in range(4):
            d = 0 if q in HALVES[ch[e][0]] else 1
            for r in cr[q]:
                ml[(e, d)] = ml.get((e, d), 0) + cnt[e][r]
                if r != e ^ 1:
                    sw[(0, e ^ 1, d)] = sw.get((0, e ^ 1, d), 0) + cnt[e][r]
                    sw[(1, r, d)] = sw.get((1, r, d), 0) + cnt[e][r]
            d = 0 if q in HALVES[ch[e][1]] else 1
            for r in sm[q]:
                sw[(0, e, d)] = sw.get((0, e, d), 0) + cnt[e][r]
                sw[(1, r, d)] = sw.get((1, r, d), 0) + cnt[e][r]
    return max(sw.values()), sum(x * x for x in sw.values()) + sum(x * x for x in ml.values())


def plan(T):
    if "ok" in PLAN:
        return PLAN
    route = T.tables["ROUTE"]
    n = len(route)
    nt = T.tables["T"]
    cnt = [[0] * n for _ in range(n)]
    for r in range(n):
        for t in range(nt):
            for e in route[r][t]:
                cnt[e][r] += 1
    off = [[0] * n for _ in range(n)]
    for e in range(n):
        s = 0
        for r in range(n):
            off[e][r] = s
            s += cnt[e][r]
    ch = []
    for e in range(n):
        rot = (e // 2) % 4
        a = HALVES.index(tuple(sorted(q for q in range(4) if (q + rot) % 4 < 2)))
        ch.append((a, a))
    for _ in range(4):
        for e in range(n):
            best = None
            for a in range(6):
                for b in range(6):
                    ch[e] = (a, b)
                    v = port_cost(ch, cnt, n)
                    if best is None or v < best[0]:
                        best = (v, (a, b))
            ch[e] = best[1]
    serve = [[[] for _ in range(8)] for _ in range(n)]
    for e in range(n):
        cr, sm = pairs_of(e)
        for prs, cores, half in ((cr, CROSS, HALVES[ch[e][0]]), (sm, SAME, HALVES[ch[e][1]])):
            order = [q for q in range(4) if q in half] + [q for q in range(4) if q not in half]
            for i, q in enumerate(order):
                serve[e][cores[i]] = prs[q]
    land = [[0] * n for _ in range(n)]
    group = [[0] * n for _ in range(n)]
    for r in range(n):
        keys = []
        for e in range(n):
            if e == r:
                keys.append((-1.0, e))
                continue
            k = [c for c in range(8) if r in serve[e][c]][0]
            key = 0.0 if k == e % 8 else (1.2 if k in CROSS else 2.0)
            key += 0.7 * serve[e][k].index(r)
            if (e & 1) != (r & 1) and (e ^ 1) != r:
                key += 0.5
            keys.append((key, e))
        s = 0
        for _, e in sorted(keys):
            land[r][e] = s
            group[r][e] = s // 128
            s += cnt[e][r]
    idx = [[[0] * 3 for _ in range(nt)] for _ in range(n)]
    for r in range(n):
        fill = [0] * n
        for t in range(nt):
            for k, e in enumerate(route[r][t]):
                idx[r][t][k] = land[r][e] + fill[e]
                fill[e] += 1
    PLAN.update(cnt=cnt, off=off, serve=serve, land=land, group=group, idx=idx, n=n, nt=nt, ok=True)
    return PLAN


def rank_program(g, core, T, topo):
    P = plan(T)
    chip, k = core // 8, core % 8
    e = chip
    rcore = T.cores[e]
    is_rank = core == rcore
    cnt, off, serve, land, group, idx = P["cnt"], P["off"], P["serve"], P["land"], P["group"], P["idx"]
    S = T.sem
    V = g.vector
    nt = P["nt"]
    role = (k - rcore % 8) % 8
    rrid, rpid, _ = topo.addr(rcore)

    if is_rank:
        g.sync.dma_start(T.zs[:], T.z[:]).then_inc(S.zld, 16)
        a = off[e][e]
        g.scalar.dma_start(T.zland[:, land[e][e]:land[e][e] + cnt[e][e]], T.z[:, a:a + cnt[e][e]]).then_inc(
            S["arr%d" % group[e][e]], 16)
    if role in (1, 2):
        buf, drm = (T.ia, T.idr) if role == 1 else (T.ib, T.ibr)
        V.memset(buf[:], 0.0).then_inc(S.ias, 1)
        V.wait_ge(S.ias, 1)
        V.memset(buf[:, 0:1], 1.0).then_inc(S.ias, 1)
        if role == 2:
            V.memset(buf[:, 128:129], -1.0).then_inc(S.ias, 1)
        g.sync.wait_ge(S.ias, role + 1)
        g.sync.dma_start(drm[:], buf[:]).then_inc(S.id1, 16)

    V.memset(T.pb[:, k], 0.0).then_inc(S.pbs, 1)
    V.wait_ge(S.pbs, 1)
    for jj in range(NP):
        j = k * NP + jj
        c = idx[e][j % nt][j // nt]
        x = (c // 128) * NP + jj
        V.memset(T.pb[0:c % 128 + 1, k, x:x + 1], 1.0).then_inc(S.pbs, 1)

    sent = 0
    if not is_rank:
        if role == 1:
            g.wait_ge(S.id1, 16)
            g.remote_dma(T.ident[:], T.idr[0:128, :], S.id2, S.sent, rpid, rrid, 0xFFFF)
            sent += 16
        if role == 2:
            g.wait_ge(S.id1, 16)
            g.remote_dma(T.dmat[:], T.ibr[0:128, :], S.ib2, S.sent, rpid, rrid, 0xFFFF)
            sent += 16
        g.wait_ge(S.pbs, NP + 1)
        g.remote_dma(T.pb[:, k], T.pb[:, k], S.parr, S.sent, rpid, rrid, 0xFFFF)
        sent += 16
        g.wait_ge(S.zarr, 4)
    else:
        g.wait_ge(S.zld, 16)
        for cores in (CROSS, SAME):
            trs = []
            for h in cores:
                if h == k:
                    continue
                ws = min(off[e][serve[e][h][0]], 401 - WD)
                rid, pid, _ = topo.addr(chip * 8 + h)
                trs.append(RemoteDMATransfer(dst_ids=[DstId(rid=rid, pnc=pid)], dma_engine_mask=15 << (4 * len(trs)),
                                             remote_sem=S.zarr, src=T.zs[:, ws:ws + WD], dst=T.zh[:]))
            g.remote_dma_fused(trs, local_sem=S.sent)
            sent += 4 * len(trs)

    ds = serve[e][k]
    ws = 0 if is_rank else min(off[e][ds[0]], 401 - WD)
    src = T.zs if is_rank else T.zh
    for d in ds:
        a = off[e][d] - ws
        w = cnt[e][d]
        rid, pid, _ = topo.addr(T.cores[d])
        g.remote_dma(T.zland[:, land[d][e]:land[d][e] + w], src[:, a:a + w], S["arr%d" % group[d][e]], S.sent,
                     pid, rid, 0x00FF)
        sent += 8
    if is_rank:
        g.sem_inc(S.go, 1)
        g.scalar.wait_ge(S.go, 1)
        g.scalar.dma_start(T.gs[:], T.g[:]).then_inc(S.gld, 16)
    g.wait_ge(S.sent, sent)
    if not is_rank:
        return

    need = [0, 0, 0]
    for s in range(P["n"]):
        need[group[e][s]] += 16 if s == e else 8
    pst = [T.pst0, T.pst1, T.pst2]
    psp = [T.psp0, T.psp1, T.psp2]
    PE = g.tensor
    PE.wait_ge(S.ib2, 16)
    PE.wait_ge(S.pbs, NP + 1)
    PE.wait_ge(S.parr, 7 * 16)
    for h in range(8):
        b, i = h // 3, h % 3
        PE.matmul(psp[b][:, i * 3 * NP:(i + 1) * 3 * NP], T.dmat[:], T.pb[:, h], start=True, stop=True).then_inc(
            S["pm%d" % b], 1)
    for h in range(8):
        b, i = h // 3, h % 3
        if i == 0:
            V.wait_ge(S["pm%d" % b], 3 if b < 2 else 2)
        V.tensor_copy(T.pf[:, :, h * NP:(h + 1) * NP], psp[b][:, i * 3 * NP:(i + 1) * 3 * NP]).then_inc(S.pfr, 1)
    PE.wait_ge(S.id2, 16)
    for ch in range(3):
        PE.wait_ge(S["arr%d" % ch], need[ch])
        PE.matmul(pst[ch][:, 0:128], T.zland[:, ch * 128:(ch + 1) * 128], T.ident[:], start=True, stop=True).then_inc(
            S.tp, 1)
        V.wait_ge(S.tp, ch + 1)
        V.tensor_copy(T.zt[:, ch], pst[ch][:, 0:128]).then_inc(S.tc, 1)
        PE.wait_ge(S.tc, ch + 1)
        if ch == 0:
            PE.wait_ge(S.pfr, 8)
        for kp in range(3):
            PE.matmul(psp[kp][:, 0:128], T.zt[:, ch], T.pf[:, ch, kp * 128:(kp + 1) * 128], start=(ch == 0),
                      stop=(ch == 2)).then_inc(S["mk%d" % kp], 1)
    V.wait_ge(S.gld, 16)
    V.wait_ge(S.mk0, 3)
    V.tensor_tensor(T.p0[:], T.gs[:, 0::3], psp[0][:, 0:128], AluOpType.mult).then_inc(S.dv, 1)
    V.wait_ge(S.mk1, 3)
    V.tensor_tensor(T.psa[:, 0:128], T.gs[:, 1::3], psp[1][:, 0:128], AluOpType.mult).then_inc(S.dv, 1)
    V.wait_ge(S.dv, 2)
    V.tensor_tensor(T.psa[:, 128:256], T.p0[:], T.psa[:, 0:128], AluOpType.add).then_inc(S.dv, 1)
    V.wait_ge(S.mk2, 3)
    V.tensor_tensor(T.p2[:], T.gs[:, 2::3], psp[2][:, 0:128], AluOpType.mult).then_inc(S.dv, 1)
    V.wait_ge(S.dv, 4)
    V.tensor_tensor(T.ys[:], T.p2[:], T.psa[:, 128:256], AluOpType.add).then_inc(S.dv, 1)
    g.sync.wait_ge(S.dv, 5)
    g.sync.dma_start(T.y[:], T.ys[:]).then_inc(S.yst, 16)
    g.sync.wait_ge(S.yst, 16)
